import numpy as np
import ml_dtypes


def mxq(x, axis, fmt="e4m3"):
    dtype, down = {"e4m3": (ml_dtypes.float8_e4m3fn, 7), "e5m2": (ml_dtypes.float8_e5m2, 14)}[fmt]
    v = np.moveaxis(np.asarray(x, np.float32).astype(ml_dtypes.bfloat16).astype(np.float64), axis, -1)
    blocks = v.reshape(v.shape[:-1] + (-1, 32))
    amax = np.abs(blocks).max(-1, keepdims=True)
    byte = np.maximum(np.where(amax > 0, np.frexp(amax)[1] - 1 + 127, 0) - down, 1)
    scale = np.exp2(byte - 127.0)
    codes = (blocks / scale).astype(np.float32).astype(dtype).astype(np.float64)
    return np.moveaxis((codes * scale).reshape(v.shape), -1, axis)


WIDE = False


def mx_kscale(k):
    if not WIDE:
        return np.ones(k)
    levels = np.array([10, -10, 5, -5, 0])
    if k % 512:
        return np.exp2(np.random.permutation(np.resize(levels, k // 32))).repeat(32)
    a = np.empty((k // 512, 16))
    for p in range(k // 512):
        a[p, :8] = np.random.permutation(np.resize(levels, 8))
        for g in range(8):
            far = levels[np.abs(levels - a[p, g]) >= 10]
            a[p, g + 8] = far[np.random.randint(len(far))]
    return np.exp2(a.ravel()).repeat(32)


def f64(x):
    return np.asarray(x).astype(np.float64)


def striped(idx):
    return np.tile(idx.reshape(-1, 16).T, (8, 1)).astype(np.uint16)


def unstriped(offs):
    return offs[:16].T.reshape(-1).astype(np.int64)


E2M1 = np.array([0.0, 0.5, 1.0, 1.5, 2.0, 3.0, 4.0, 6.0, -0.0, -0.5, -1.0, -1.5, -2.0, -3.0, -4.0, -6.0])


def pack_weight(w, fmt):
    k, n = w.shape
    w = f64(np.asarray(w, np.float32).astype(ml_dtypes.bfloat16)).reshape(k // 32, 32, n)
    amax = np.abs(w).max(1)
    if fmt == "e4m3":
        byte = np.frexp(amax)[1] - 1 + 127 - 7
    else:
        mant, ex = np.frexp(amax / 6.0)
        byte = np.where(mant > 0.5, ex, ex - 1) + 127
    byte = np.clip(np.where(amax > 0, byte, 1), 1, 254)
    scaled = (w * np.exp2(127.0 - byte)[:, None, :]).reshape(k, n).astype(np.float32)
    by_word = np.ascontiguousarray(scaled.reshape(k // 512, 128, 4, n).transpose(0, 1, 3, 2))
    if fmt == "e4m3":
        words = by_word.astype(ml_dtypes.float8_e4m3fn).view(np.uint8)
    else:
        c = by_word.astype(ml_dtypes.float4_e2m1fn).view(np.uint8) & 0xF
        words = (c[..., 0::2] | (c[..., 1::2] << 4)).reshape(k // 512, 128, 2 * n)
    return np.ascontiguousarray(words), np.ascontiguousarray(byte.astype(np.uint8).reshape(k // 512, 16, n))


def unpack_weight(words, scales, fmt):
    g, _, n = scales.shape
    words = np.ascontiguousarray(words).reshape(g, 128, n, -1)
    if fmt == "e4m3":
        vals = words.view(ml_dtypes.float8_e4m3fn).astype(np.float64)
    else:
        nib = np.empty((g, 128, n, 4), np.uint8)
        nib[..., 0::2] = words & 0xF
        nib[..., 1::2] = words >> 4
        vals = E2M1[nib]
    vals = vals * np.repeat(np.exp2(scales.astype(np.float64) - 127.0), 8, axis=1)[..., None]
    return vals.transpose(0, 1, 3, 2).reshape(g * 512, n)


K, T, E, C, N = 256, 1536, 24, 128, 512


def by_expert(wq, xq):
    return np.concatenate([wq[e].T @ xq[:, e * C:(e + 1) * C] for e in range(E)], axis=1)


def setup_inputs():
    n = np.random.standard_normal
    s = mx_kscale(N)[:, None]
    first = np.random.permutation(np.repeat(np.arange(E), T // E))
    second = (first + 1 + np.random.permutation(np.repeat(np.arange(E - 1), -(-T // (E - 1)))[:T])) % E
    while np.bincount(second, minlength=E).max() != T // E:
        load = np.bincount(second, minlength=E); hi, lo = int(load.argmax()), int(load.argmin())
        t = np.flatnonzero((second == hi) & (first != lo))[0]; second[t] = lo
    slot_token = np.empty(E * C, np.int64); pos = np.empty((2, T), np.int64); fill = np.zeros(E, np.int64)
    place = np.stack([np.random.permutation(C) for _ in range(E)])
    for r, deal in enumerate((first, second)):
        for t in np.random.permutation(T):
            e = deal[t]; j = e * C + place[e, fill[e]]; fill[e] += 1; slot_token[j] = t; pos[r, t] = j
    g = np.random.uniform(0.2, 0.8, T)
    w_slot = np.empty(E * C); w_slot[pos[0]] = g; w_slot[pos[1]] = 1.0 - g
    w = [pack_weight(m, "e2m1") for m in n((E, N, K)) / np.sqrt(N) / s[None]]
    return {
        "dyT": (n((N, T)) * s).astype(np.float32),
        "w_words": np.stack([m[0] for m in w]),
        "w_scales": np.stack([m[1] for m in w]),
        "gate": np.tile(w_slot, (N, 1)).astype(np.float32),
        "offs": striped(slot_token),
        "pos1": striped(pos[0]),
        "pos2": striped(pos[1]),
    }


def reference(dyT, w_words, w_scales, gate, offs, pos1, pos2):
    idx = unstriped(offs)
    w = np.stack([unpack_weight(w_words[e], w_scales[e], "e2m1") for e in range(E)])
    gq = mxq(f64(gate) * f64(dyT)[:, idx], 0, "e4m3")
    dx = by_expert(w, gq)
    return dx[:, unstriped(pos1)] + dx[:, unstriped(pos2)]

@@ -1,0 +1,149 @@
+from contextlib import ExitStack
+
+import concourse.mybir as mybir
+
+N, T, E, C, K = 512, 1536, 24, 128, 256
+S = E * C
+
+F32 = mybir.dt.float32
+BF16 = mybir.dt.bfloat16
+U32 = mybir.dt.uint32
+I32 = mybir.dt.int32
+U16 = mybir.dt.uint16
+U8 = mybir.dt.uint8
+FP8X4 = mybir.dt.float8_e4m3fn_x4
+FP4X4 = mybir.dt.float4_e2m1fn_x4
+MULT = mybir.AluOpType.mult
+ADD = mybir.AluOpType.add
+
+FLOPS = 2 * N * K * S
+BYTES = 4 * N * T + E * N * K // 2 + E * 16 * K + 4 * S + 2 * 128 * (S // 16 + 2 * (T // 16)) + 4 * K * T
+
+P = 128
+PACK = 4
+HALVES = K // P
+
+CHUNKS = (1024, 1024, 512, 256, 128, 128)
+PIECES = ((0, 0, 1536), (1, 0, 768), (1, 768, 384), (1, 1152, 384))
+
+
+def tile_moe_bdx_lin_none_kernel(tc, dyT, w_words, w_scales, gate, offs, pos1, pos2, out):
+    nc = tc.nc
+    with ExitStack() as ctx:
+        lists = ctx.enter_context(tc.tile_pool(name="lists", bufs=1))
+        keep = ctx.enter_context(tc.tile_pool(name="keep", bufs=1))
+        work = ctx.enter_context(tc.tile_pool(name="work", bufs=3))
+        ends = ctx.enter_context(tc.tile_pool(name="ends", bufs=4))
+        psum = ctx.enter_context(tc.psum_pool(name="psum", bufs=8))
+
+        offs_t = lists.tile([P, S // 16], U16, name="offs_t")
+        pos1_t = lists.tile([P, T // 16], U16, name="pos1_t")
+        pos2_t = lists.tile([P, T // 16], U16, name="pos2_t")
+
+        planes = [keep.tile([P, T], F32, name=f"plane{t}") for t in range(PACK)]
+        gates = keep.tile([P, S], F32, name="gates")
+        words = keep.tile([P, E * 2 * K], U8, name="words", align_bytes=64)
+        wscale = keep.tile([P, E * K], U8, name="wscale", align_bytes=64)
+        dx = [keep.tile([P, S], F32, name=f"dx{h}") for h in range(HALVES)]
+
+        nc.vector.memset(wscale[:].bitcast(I32), 0)
+
+        dyT_rows = dyT.rearrange("(p j) t -> p j t", j=PACK)
+        nc.sync.dma_start(offs_t[:], offs)
+        nc.sync.dma_start(gates[:, 0:512], gate[0:P, 0:512])
+        nc.sync.dma_start(planes[0][:], dyT_rows[:, 0, :])
+        nc.sync.dma_start(gates[:, 512:1024], gate[0:P, 512:1024])
+        for t in range(1, PACK):
+            nc.sync.dma_start(planes[t][:], dyT_rows[:, t, :])
+        nc.sync.dma_start(gates[:, 1024:2048], gate[0:P, 1024:2048])
+        for q in range(4):
+            nc.sync.dma_start(
+                wscale[32 * q : 32 * q + 4, :].bitcast(I32).rearrange("p (e k) -> p e k", e=E),
+                w_scales[:, 0, 4 * q : 4 * q + 4, :].bitcast(I32).rearrange("e f k -> f e k"),
+            )
+        def load_words(e0, e1):
+            nc.sync.dma_start(
+                words[:, e0 * 2 * K : e1 * 2 * K].bitcast(I32).rearrange("p (e k) -> p e k", e=e1 - e0),
+                w_words[e0:e1, 0, :, :].bitcast(I32).rearrange("e p k -> p e k"),
+            )
+        load_words(0, 8)
+        nc.sync.dma_start(gates[:, 2048:3072], gate[0:P, 2048:3072])
+        load_words(8, 16)
+        load_words(16, 24)
+        nc.sync.dma_start(pos1_t[:], pos1)
+        nc.sync.dma_start(pos2_t[:], pos2)
+
+        def gather(start, n):
+            g4 = work.tile([P, PACK, n], F32, name="g4", align_bytes=64)
+            for t in range(PACK):
+                cuts = ((0, 512), (512, 1024)) if start == 0 and t == 0 else ((0, n),)
+                for a, b in cuts:
+                    nc.vector.tensor_tensor(
+                        g4[:, t, a:b],
+                        planes[t][:].indirect(offs_t[:, (start + a) // 16 : (start + b) // 16]),
+                        gates[:, start + a : start + b],
+                        MULT,
+                    )
+            return g4
+
+        def interleave(g4, n, last):
+            grouped = work.tile([P, n, PACK], BF16, name="grouped", align_bytes=64)
+            turned = g4[:].rearrange("p t n -> p n t")
+            if last:
+                nc.scalar.copy(grouped[:, :, 0:2], turned[:, :, 0:2])
+                nc.vector.tensor_copy(grouped[:, :, 2:4], turned[:, :, 2:4])
+            else:
+                nc.scalar.copy(grouped[:], turned)
+            return grouped
+
+        def multiply(grouped, start, n):
+            codes = work.tile([P, n], U32, name="codes", align_bytes=64)
+            scales = work.tile([P, n], U8, name="scales", align_bytes=64)
+            nc.vector.quantize_mx(
+                out=codes[:].bitcast(FP8X4),
+                scales=scales[:],
+                in_=grouped[:].rearrange("p n t -> p (n t)"),
+            )
+            for b0 in range(0, n, 512):
+                width = min(512, n - b0)
+                for h in range(HALVES):
+                    bank = psum.tile([P, 512], F32, name="bank")
+                    for c in range(0, width, C):
+                        e = (start + b0 + c) // C
+                        col = e * K + h * P
+                        nc.tensor.matmul_mx(
+                            out=bank[:, c : c + C],
+                            lhsT=words[:, 2 * col : 2 * (col + P)].bitcast(FP4X4),
+                            lhsT_scale=wscale[:, col : col + P],
+                            rhs=codes[:, b0 + c : b0 + c + C].bitcast(FP8X4),
+                            rhs_scale=scales[:, b0 + c : b0 + c + C],
+                            start=True,
+                            stop=True,
+                        )
+                    target = dx[h][:, start + b0 : start + b0 + width]
+                    if h == 0 and start + n == S:
+                        nc.vector.tensor_copy(target, bank[:, 0:width])
+                    else:
+                        nc.scalar.copy(target, bank[:, 0:width])
+
+        start = 0
+        waiting = None
+        for n in CHUNKS:
+            g4 = gather(start, n)
+            grouped = interleave(g4, n, start + n == S)
+            if waiting is not None:
+                multiply(*waiting)
+            waiting = (grouped, start, n)
+            start += n
+        multiply(*waiting)
+
+        for i, (h, t0, n) in enumerate(PIECES):
+            picked = []
+            for name, pos in (("first", pos1_t), ("second", pos2_t)):
+                got = ends.tile([P, n], F32, name=name)
+                nc.vector.tensor_copy(got[:], dx[h][:].indirect(pos[:, t0 // 16 : (t0 + n) // 16]))
+                picked.append(got)
+            total = ends.tile([P, n], F32, name="total")
+            engine = nc.vector if i == len(PIECES) - 1 else nc.gpsimd
+            engine.tensor_tensor(total[:], picked[0][:], picked[1][:], ADD)
+            nc.sync.dma_start(out[h * P : (h + 1) * P, t0 : t0 + n], total[:])

@@ -23,8 +23,9 @@ P = 128
 PACK = 4
 HALVES = K // P
 
-CHUNKS = (1024, 1024, 512, 256, 128, 128)
-PIECES = ((0, 0, 1536), (1, 0, 768), (1, 768, 384), (1, 1152, 384))
+CHUNKS = (1024, 512, 512, 512, 256, 256)
+AFTER = {(2, 0): (0,), (2, 1): (1,), (3, 2): (2,), (5, 0): (3,), (5, 2): (4,)}
+PIECES = ((0, 0, 1536, ((0, 1536),)), (1, 0, 768, ((0, 768),)), (1, 768, 768, ((0, 384), (384, 768))))
 
 
 def tile_moe_bdx_lin_none_kernel(tc, dyT, w_words, w_scales, gate, offs, pos1, pos2, out):
@@ -33,7 +34,7 @@ def tile_moe_bdx_lin_none_kernel(tc, dyT, w_words, w_scales, gate, offs, pos1, p
         lists = ctx.enter_context(tc.tile_pool(name="lists", bufs=1))
         keep = ctx.enter_context(tc.tile_pool(name="keep", bufs=1))
         work = ctx.enter_context(tc.tile_pool(name="work", bufs=3))
-        ends = ctx.enter_context(tc.tile_pool(name="ends", bufs=4))
+        ends = ctx.enter_context(tc.tile_pool(name="ends", bufs=3))
         psum = ctx.enter_context(tc.psum_pool(name="psum", bufs=8))
 
         offs_t = lists.tile([P, S // 16], U16, name="offs_t")
@@ -50,9 +51,9 @@ def tile_moe_bdx_lin_none_kernel(tc, dyT, w_words, w_scales, gate, offs, pos1, p
 
         dyT_rows = dyT.rearrange("(p j) t -> p j t", j=PACK)
         nc.sync.dma_start(offs_t[:], offs)
-        nc.sync.dma_start(gates[:, 0:512], gate[0:P, 0:512])
+        nc.sync.dma_start(gates[:, 0:256], gate[0:P, 0:256])
         nc.sync.dma_start(planes[0][:], dyT_rows[:, 0, :])
-        nc.sync.dma_start(gates[:, 512:1024], gate[0:P, 512:1024])
+        nc.sync.dma_start(gates[:, 256:1024], gate[0:P, 256:1024])
         for t in range(1, PACK):
             nc.sync.dma_start(planes[t][:], dyT_rows[:, t, :])
         nc.sync.dma_start(gates[:, 1024:2048], gate[0:P, 1024:2048])
@@ -73,10 +74,9 @@ def tile_moe_bdx_lin_none_kernel(tc, dyT, w_words, w_scales, gate, offs, pos1, p
         nc.sync.dma_start(pos1_t[:], pos1)
         nc.sync.dma_start(pos2_t[:], pos2)
 
-        def gather(start, n):
-            g4 = work.tile([P, PACK, n], F32, name="g4", align_bytes=64)
-            for t in range(PACK):
-                cuts = ((0, 512), (512, 1024)) if start == 0 and t == 0 else ((0, n),)
+        def gather(g4, t, start, n):
+            if True:
+                cuts = ((0, 256), (256, n)) if start == 0 and t == 0 else ((0, n),)
                 for a, b in cuts:
                     nc.vector.tensor_tensor(
                         g4[:, t, a:b],
@@ -84,16 +84,13 @@ def tile_moe_bdx_lin_none_kernel(tc, dyT, w_words, w_scales, gate, offs, pos1, p
                         gates[:, start + a : start + b],
                         MULT,
                     )
-            return g4
 
-        def interleave(g4, n, last):
+        def interleave(g4, n):
             grouped = work.tile([P, n, PACK], BF16, name="grouped", align_bytes=64)
-            turned = g4[:].rearrange("p t n -> p n t")
-            if last:
-                nc.scalar.copy(grouped[:, :, 0:2], turned[:, :, 0:2])
-                nc.vector.tensor_copy(grouped[:, :, 2:4], turned[:, :, 2:4])
-            else:
-                nc.scalar.copy(grouped[:], turned)
+            nc.scalar.copy(
+                grouped[:].rearrange("p (c i) t -> p c t i", i=4),
+                g4[:].rearrange("p t (c i) -> p c t i", i=4),
+            )
             return grouped
 
         def multiply(grouped, start, n):
@@ -126,24 +123,37 @@ def tile_moe_bdx_lin_none_kernel(tc, dyT, w_words, w_scales, gate, offs, pos1, p
                     else:
                         nc.scalar.copy(target, bank[:, 0:width])
 
-        start = 0
-        waiting = None
-        for n in CHUNKS:
-            g4 = gather(start, n)
-            grouped = interleave(g4, n, start + n == S)
-            if waiting is not None:
-                multiply(*waiting)
-            waiting = (grouped, start, n)
-            start += n
-        multiply(*waiting)
+        starts = [sum(CHUNKS[:c]) for c in range(len(CHUNKS))]
+        grouped = {}
+        for c, (start, n) in enumerate(zip(starts, CHUNKS)):
+            g4 = work.tile([P, PACK, n], F32, name="g4", align_bytes=64)
+            for t in range(PACK):
+                gather(g4, t, start, n)
+                if start + n == S and t % 2 == 1:
+                    if t == 1:
+                        grouped[c] = work.tile([P, n, PACK], BF16, name="grouped", align_bytes=64)
+                    copy = nc.scalar.copy if t == 1 else nc.vector.tensor_copy
+                    copy(grouped[c][:, :, t - 1 : t + 1], g4[:].rearrange("p t n -> p n t")[:, :, t - 1 : t + 1])
+                for b in AFTER.get((c, t), ()):
+                    multiply(grouped[b], starts[b], CHUNKS[b])
+            if start + n < S:
+                grouped[c] = interleave(g4, n)
+        multiply(grouped[c], start, n)
 
-        for i, (h, t0, n) in enumerate(PIECES):
-            picked = []
-            for name, pos in (("first", pos1_t), ("second", pos2_t)):
-                got = ends.tile([P, n], F32, name=name)
-                nc.vector.tensor_copy(got[:], dx[h][:].indirect(pos[:, t0 // 16 : (t0 + n) // 16]))
-                picked.append(got)
+        def fetch(h, pos, t0, n, name):
+            got = ends.tile([P, n], F32, name=name)
+            nc.vector.tensor_copy(got[:], dx[h][:].indirect(pos[:, t0 // 16 : (t0 + n) // 16]))
+            return got
+
+        def add(engine, h, t0, first, second):
+            n = second.shape[1]
             total = ends.tile([P, n], F32, name="total")
-            engine = nc.vector if i == len(PIECES) - 1 else nc.gpsimd
-            engine.tensor_tensor(total[:], picked[0][:], picked[1][:], ADD)
+            engine.tensor_tensor(total[:], first, second[:], ADD)
             nc.sync.dma_start(out[h * P : (h + 1) * P, t0 : t0 + n], total[:])
+
+        for h, t0, n, cuts in PIECES:
+            first = fetch(h, pos1_t, t0, n, "first")
+            for a, b in cuts:
+                second = fetch(h, pos2_t, t0 + a, b - a, "second")
+                engine = nc.vector if h == 1 and t0 + b == T else nc.gpsimd
+                add(engine, h, t0 + a, first[:, a:b], second)

from contextlib import ExitStack

import concourse.mybir as mybir

N, T, E, C, K = 512, 1536, 24, 128, 256
S = E * C

F32 = mybir.dt.float32
BF16 = mybir.dt.bfloat16
U32 = mybir.dt.uint32
I32 = mybir.dt.int32
U16 = mybir.dt.uint16
U8 = mybir.dt.uint8
FP8X4 = mybir.dt.float8_e4m3fn_x4
FP4X4 = mybir.dt.float4_e2m1fn_x4
MULT = mybir.AluOpType.mult
ADD = mybir.AluOpType.add

FLOPS = 2 * N * K * S
BYTES = 4 * N * T + E * N * K // 2 + E * 16 * K + 4 * S + 2 * 128 * (S // 16 + 2 * (T // 16)) + 4 * K * T

P = 128
PACK = 4
HALVES = K // P

CHUNKS = (1024, 512, 512, 512, 256, 256)
AFTER = {(2, 0): (0,), (2, 1): (1,), (3, 2): (2,), (5, 0): (3,), (5, 2): (4,)}
PIECES = ((0, 0, 1536, ((0, 1536),)), (1, 0, 768, ((0, 768),)), (1, 768, 768, ((0, 384), (384, 768))))


def tile_moe_bdx_lin_none_kernel(tc, dyT, w_words, w_scales, gate, offs, pos1, pos2, out):
    nc = tc.nc
    with ExitStack() as ctx:
        lists = ctx.enter_context(tc.tile_pool(name="lists", bufs=1))
        keep = ctx.enter_context(tc.tile_pool(name="keep", bufs=1))
        work = ctx.enter_context(tc.tile_pool(name="work", bufs=3))
        ends = ctx.enter_context(tc.tile_pool(name="ends", bufs=3))
        psum = ctx.enter_context(tc.psum_pool(name="psum", bufs=8))

        offs_t = lists.tile([P, S // 16], U16, name="offs_t")
        pos1_t = lists.tile([P, T // 16], U16, name="pos1_t")
        pos2_t = lists.tile([P, T // 16], U16, name="pos2_t")

        planes = [keep.tile([P, T], F32, name=f"plane{t}") for t in range(PACK)]
        gates = keep.tile([P, S], F32, name="gates")
        words = keep.tile([P, E * 2 * K], U8, name="words", align_bytes=64)
        wscale = keep.tile([P, E * K], U8, name="wscale", align_bytes=64)
        dx = [keep.tile([P, S], F32, name=f"dx{h}") for h in range(HALVES)]

        nc.vector.memset(wscale[:].bitcast(I32), 0)

        dyT_rows = dyT.rearrange("(p j) t -> p j t", j=PACK)
        nc.sync.dma_start(offs_t[:], offs)
        nc.sync.dma_start(gates[:, 0:256], gate[0:P, 0:256])
        nc.sync.dma_start(planes[0][:], dyT_rows[:, 0, :])
        nc.sync.dma_start(gates[:, 256:1024], gate[0:P, 256:1024])
        for t in range(1, PACK):
            nc.sync.dma_start(planes[t][:], dyT_rows[:, t, :])
        nc.sync.dma_start(gates[:, 1024:2048], gate[0:P, 1024:2048])
        for q in range(4):
            nc.sync.dma_start(
                wscale[32 * q : 32 * q + 4, :].bitcast(I32).rearrange("p (e k) -> p e k", e=E),
                w_scales[:, 0, 4 * q : 4 * q + 4, :].bitcast(I32).rearrange("e f k -> f e k"),
            )
        def load_words(e0, e1):
            nc.sync.dma_start(
                words[:, e0 * 2 * K : e1 * 2 * K].bitcast(I32).rearrange("p (e k) -> p e k", e=e1 - e0),
                w_words[e0:e1, 0, :, :].bitcast(I32).rearrange("e p k -> p e k"),
            )
        load_words(0, 8)
        nc.sync.dma_start(gates[:, 2048:3072], gate[0:P, 2048:3072])
        load_words(8, 16)
        load_words(16, 24)
        nc.sync.dma_start(pos1_t[:], pos1)
        nc.sync.dma_start(pos2_t[:], pos2)

        def gather(g4, t, start, n):
            if True:
                cuts = ((0, 256), (256, n)) if start == 0 and t == 0 else ((0, n),)
                for a, b in cuts:
                    nc.vector.tensor_tensor(
                        g4[:, t, a:b],
                        planes[t][:].indirect(offs_t[:, (start + a) // 16 : (start + b) // 16]),
                        gates[:, start + a : start + b],
                        MULT,
                    )

        def interleave(g4, n):
            grouped = work.tile([P, n, PACK], BF16, name="grouped", align_bytes=64)
            nc.scalar.copy(
                grouped[:].rearrange("p (c i) t -> p c t i", i=4),
                g4[:].rearrange("p t (c i) -> p c t i", i=4),
            )
            return grouped

        def multiply(grouped, start, n):
            codes = work.tile([P, n], U32, name="codes", align_bytes=64)
            scales = work.tile([P, n], U8, name="scales", align_bytes=64)
            nc.vector.quantize_mx(
                out=codes[:].bitcast(FP8X4),
                scales=scales[:],
                in_=grouped[:].rearrange("p n t -> p (n t)"),
            )
            for b0 in range(0, n, 512):
                width = min(512, n - b0)
                for h in range(HALVES):
                    bank = psum.tile([P, 512], F32, name="bank")
                    for c in range(0, width, C):
                        e = (start + b0 + c) // C
                        col = e * K + h * P
                        nc.tensor.matmul_mx(
                            out=bank[:, c : c + C],
                            lhsT=words[:, 2 * col : 2 * (col + P)].bitcast(FP4X4),
                            lhsT_scale=wscale[:, col : col + P],
                            rhs=codes[:, b0 + c : b0 + c + C].bitcast(FP8X4),
                            rhs_scale=scales[:, b0 + c : b0 + c + C],
                            start=True,
                            stop=True,
                        )
                    target = dx[h][:, start + b0 : start + b0 + width]
                    if h == 0 and start + n == S:
                        nc.vector.tensor_copy(target, bank[:, 0:width])
                    else:
                        nc.scalar.copy(target, bank[:, 0:width])

        starts = [sum(CHUNKS[:c]) for c in range(len(CHUNKS))]
        grouped = {}
        for c, (start, n) in enumerate(zip(starts, CHUNKS)):
            g4 = work.tile([P, PACK, n], F32, name="g4", align_bytes=64)
            for t in range(PACK):
                gather(g4, t, start, n)
                if start + n == S and t % 2 == 1:
                    if t == 1:
                        grouped[c] = work.tile([P, n, PACK], BF16, name="grouped", align_bytes=64)
                    copy = nc.scalar.copy if t == 1 else nc.vector.tensor_copy
                    copy(grouped[c][:, :, t - 1 : t + 1], g4[:].rearrange("p t n -> p n t")[:, :, t - 1 : t + 1])
                for b in AFTER.get((c, t), ()):
                    multiply(grouped[b], starts[b], CHUNKS[b])
            if start + n < S:
                grouped[c] = interleave(g4, n)
        multiply(grouped[c], start, n)

        def fetch(h, pos, t0, n, name):
            got = ends.tile([P, n], F32, name=name)
            nc.vector.tensor_copy(got[:], dx[h][:].indirect(pos[:, t0 // 16 : (t0 + n) // 16]))
            return got

        def add(engine, h, t0, first, second):
            n = second.shape[1]
            total = ends.tile([P, n], F32, name="total")
            engine.tensor_tensor(total[:], first, second[:], ADD)
            nc.sync.dma_start(out[h * P : (h + 1) * P, t0 : t0 + n], total[:])

        for h, t0, n, cuts in PIECES:
            first = fetch(h, pos1_t, t0, n, "first")
            for a, b in cuts:
                second = fetch(h, pos2_t, t0 + a, b - a, "second")
                engine = nc.vector if h == 1 and t0 + b == T else nc.gpsimd
                add(engine, h, t0 + a, first[:, a:b], second)
